import numpy as np
CORES = [2,34,66,98,130,162,194,226,258,290,322,354,386,418,450,482]
N = 16
R, T = 4096, 128
CAPP = 32
def entries(a): return a.T.reshape(-1)
def pack(v, P): return np.ascontiguousarray(np.asarray(v, np.int32).reshape(-1, P).T)
def lists(rng, how):
    I = rng.integers(0, N * R, (N, T))
    O = np.stack([rng.permutation(np.repeat(np.arange(N), CAPP))[:T] for r in range(N)])
    if how == "full": O = np.stack([rng.permutation(np.repeat(rng.permutation(N)[:T // CAPP], CAPP)) for r in range(N)])
    I = R * O + rng.integers(0, R, (N, T))
    if how == "alike": I = R * O + rng.integers(0, R)
    if how == "edge": I = R * O + np.where(rng.random((N, T)) < 0.5, 0, R - 1)
    if how == "sorted": I = np.sort(I, axis=1)
    return {"idx": np.stack([pack(I[r], 16) for r in range(N)])}
def setup_inputs(rng):
    return dict({"gr": rng.standard_normal((N, 128, T), dtype=np.float32)}, **lists(rng, "uniform"))
def setup_inputs_alike(rng):
    d = setup_inputs(rng); d.update(lists(rng, "alike"))
    for k in ("gr",): d[k] = (d[k].astype(np.float32) * 1024.0).astype(d[k].dtype)
    return d
def setup_inputs_edge(rng):
    d = setup_inputs(rng); d.update(lists(rng, "edge"))
    for k in ("gr",): d[k] = (d[k].astype(np.float32) * (1 / 1024.0)).astype(d[k].dtype)
    return d
def setup_inputs_full(rng):
    d = setup_inputs(rng); d.update(lists(rng, "full"))
    return d
def setup_inputs_sorted(rng):
    d = setup_inputs(rng); d.update(lists(rng, "sorted"))
    return d
def check_inputs(x):
    bad = []
    if x["idx"].min() < 0 or x["idx"].max() >= N * R: bad.append("idx out of range")
    if max(int(np.bincount(entries(a) // R, minlength=N).max()) for a in x["idx"]) > CAPP: bad.append("more than CAPP entries of a list point into one rank's part")
    return bad
def reference(gr, idx):
    A = np.zeros((128, N * R))
    for r in range(N):
        np.add.at(A.T, entries(idx[r]), gr[r].astype(np.float64).T)
    return {"y": np.stack([A[:, R * r:R * r + R] for r in range(N)]).astype(np.float32)}

@@ -1,0 +1,246 @@
+from concourse.mybir import dt, AluOpType, AxisListType, ActivationFunctionType
+
+HELP = False
+W = 34
+NS = 8 * W
+RR = 4096
+YW = RR + 32
+
+F, I32, BF = "float32", "int32", "bfloat16"
+SCRATCH = {
+    "IOT": ("sbuf", [128, NS], F), "PC": ("sbuf", [128, 1], F), "QROW": ("sbuf", [128, 128], F),
+    "PAT": ("sbuf", [128, 256], F), "PI": ("sbuf", [128, 1], I32), "P16I": ("sbuf", [128, 1], I32),
+    "P16F": ("sbuf", [128, 2], F), "ONES": ("sbuf", [128, 128], F), "IDN": ("sbuf", [128, 128], F),
+    "PM": ("sbuf", [128, 128], F), "KC": ("sbuf", [128, 16], BF), "TR": ("sbuf", [128, NS], F),
+    "LAND": ("sbuf", [128, 16 * W], F), "OFFU": ("sbuf", [128, 32], "uint16"), "TMP": ("sbuf", [128, 32], F),
+    "Y": ("sbuf", [128, YW], F),
+}
+for _x in "ab":
+    SCRATCH.update({
+        "MI" + _x: ("sbuf", [128, 1], I32), "G" + _x: ("sbuf", [128, 128], F), "OI" + _x: ("sbuf", [128, 1], I32),
+        "LI" + _x: ("sbuf", [128, 1], I32), "KEY" + _x: ("sbuf", [128, 4], F), "C0" + _x: ("sbuf", [128, 8], F),
+        "DK" + _x: ("sbuf", [128, 128], F), "AA" + _x: ("sbuf", [128, 384], BF), "SEL" + _x: ("sbuf", [128, NS], F),
+        "LL" + _x: ("sbuf", [128, 256], F), "VV" + _x: ("sbuf", [128, 1], F), "RM" + _x: ("sbuf", [128, 8], F),
+        "GT" + _x: ("sbuf", [128, 128], F), "PAY" + _x: ("sbuf", [128, NS], F),
+        "RB" + _x: ("psum", [128, 512], F), "SS" + _x: ("psum", [128, 512], F),
+        "GP" + _x: ("psum", [128, 512], F), "PK" + _x: ("psum", [128, 512], F),
+    })
+SEMAPHORES = ["v", "t", "s", "gi", "ldi", "ldg", "sty", "sent", "rawi", "rawg"] + ["arr%d" % k for k in range(16)]
+
+
+def _helper(topo, c):
+    same = [x for x in range(max(0, c - 8), c + 9)
+            if x != c and topo.host(x) == topo.host(c) and topo.chip(x) == topo.chip(c)]
+    return [x for x in same if topo.die(x) != topo.die(c)][0]
+
+
+def rank_program(g, core, T, topo):
+    A = AluOpType
+    cores = list(T.cores)
+    worker = [(_helper(topo, c) if HELP else c) for c in cores]
+    rank = T.rank_of(core)
+    wrank = worker.index(core) if core in worker else None
+    if rank is None and wrank is None:
+        return
+    me = rank if rank is not None else wrank
+    home = cores[me]
+    myrack = topo.rack(topo.host(home))
+    mates = [i for i in range(len(cores)) if topo.rack(topo.host(cores[i])) == myrack]
+    rb = mates[0]
+    assert mates == list(range(rb, rb + 8))
+    partner = [i for i in range(len(cores)) if i not in mates and topo.may_write(home, cores[i])
+               and topo.chip(cores[i]) == topo.chip(home)][0]
+    a_me = me - rb
+
+    Q = {"v": g.vector, "t": g.tensor, "s": g.scalar, "g": g, "y": g.sync}
+    OWN = {"v": "v", "t": "t", "s": "s", "g": "gi"}
+    cnt, seen = {}, {}
+
+    def wait(q, tok):
+        if tok is None:
+            return
+        name, val = tok
+        if seen.get((q, name), 0) < val:
+            Q[q].wait_ge(T.sem[name], val)
+            seen[(q, name)] = val
+
+    def op(q, deps, fn):
+        own = OWN[q]
+        for d in deps:
+            wait(q, d)
+        if cnt.get(own, 0):
+            wait(q, (own, cnt[own]))
+        fn().then_inc(T.sem[own], 1)
+        cnt[own] = cnt.get(own, 0) + 1
+        return (own, cnt[own])
+
+    def neng(src, dst):
+        return bin(topo.mask(src, dst)).count("1")
+
+    def send(dst, out_ap, in_ap, rsem):
+        rid, pid = topo.addr(dst, core)
+        g.remote_dma(out_ap=out_ap, in_ap=in_ap, remote_sem=T.sem[rsem], local_sem=T.sem.sent, pid=pid,
+                     routing_id=rid, dma_engine_mask=topo.mask(core, dst))
+        cnt["sent"] = cnt.get("sent", 0) + neng(core, dst)
+
+    def expect(name, n):
+        cnt[name] = cnt.get(name, 0) + n
+        return (name, cnt[name])
+
+    V = g.vector
+    ts = V.tensor_scalar
+    sets = ("a" if rank is not None else "") + ("b" if wrank is not None else "")
+
+    tok_i = {}
+    tok_g = {}
+    if rank is not None:
+        g.sync.dma_start(T.MIa[:, 0:1], T.idx[:]).then_inc(T.sem.ldi, 16)
+        g.sync.dma_start(T.Ga[:], T.gr[:]).then_inc(T.sem.ldg, 16)
+        tok_i["a"] = expect("ldi", 16)
+        tok_g["a"] = expect("ldg", 16)
+    if wrank is not None:
+        tok_i["b"] = expect("rawi", neng(cores[partner], core))
+        tok_g["b"] = expect("rawg", neng(cores[partner], core))
+
+    op("g", [], lambda: g.iota(T.PC[:], [[0, 1]], 0, 1, allow_small_or_imprecise_dtypes=True))
+    gq = op("g", [], lambda: g.iota(T.QROW[:], [[1, 8], [8, 16]], 0, 0, allow_small_or_imprecise_dtypes=True))
+    gio = op("g", [], lambda: g.iota(T.IOT[:], [[1, NS]], 0, 0, allow_small_or_imprecise_dtypes=True))
+    op("g", [], lambda: g.iota(T.PAT[:], [[16, 2], [0, 8], [1, 16]], 0, 0, allow_small_or_imprecise_dtypes=True))
+    gall = op("g", [], lambda: g.iota(T.PI[:], [[0, 1]], 0, 1))
+
+    op("v", [], lambda: V.memset(T.ONES[:], 1.0))
+    op("v", [gq], lambda: ts(T.PM[:], T.QROW[:], T.PC[:, 0:1], None, A.is_equal))
+    for x in sets:
+        op("v", [], lambda: V.memset(T["C0" + x][:], 0.0))
+    op("v", [gio], lambda: ts(T.IDN[:], T.IOT[:, 0:128], T.PC[:, 0:1], None, A.is_equal))
+    op("v", [], lambda: V.memset(T.KC[:], 0.0))
+    op("v", [], lambda: V.memset(T.KC[:, 0:2], -1.0))
+    op("v", [], lambda: V.memset(T.KC[:, 2:3], 1.0))
+    op("v", [], lambda: V.memset(T.KC[:, 5:7], 1.0))
+    op("v", [], lambda: V.memset(T.KC[:, 7:9], -1.0))
+    op("v", [], lambda: V.memset(T.KC[:, 13:14], 1.0))
+    op("v", [], lambda: V.memset(T.TR[:], 0.0))
+    op("v", [gall], lambda: ts(T.P16I[:], T.PI[:], 15, None, A.bitwise_and))
+    op("v", [], lambda: ts(T.P16F[:, 0:1], T.P16I[:], float(RR), None, A.add))
+    op("v", [], lambda: ts(T.P16F[:, 1:2], T.P16I[:], float(RR + 16), None, A.add))
+    op("v", [], lambda: ts(T.TR[:, 32:NS:W], T.IOT[:, 0:8], 0.0, T.P16F[:, 0:1], A.mult, A.add))
+    vconst = op("v", [], lambda: ts(T.TR[:, 33:NS:W], T.IOT[:, 0:8], 0.0, T.P16F[:, 1:2], A.mult, A.add))
+
+    zero = None
+    if rank is not None:
+        cp = ActivationFunctionType.Copy
+        op("s", [gio], lambda: g.scalar.activation(T.Y[:, 0:NS], T.IOT[:], cp, scale=0.0))
+        have = NS
+        while have < YW:
+            n = min(have, YW - have)
+            zero = op("s", [], lambda: g.scalar.activation(T.Y[:, have:have + n], T.Y[:, 0:n], cp))
+            have += n
+
+    if rank is not None:
+        dst = worker[partner]
+        wait("g", tok_i["a"])
+        send(dst, T.MIb[:], T.MIa[:], "rawi")
+        wait("g", tok_g["a"])
+        send(dst, T.Gb[:], T.Ga[:], "rawg")
+
+    st = {}
+
+    def stage1(x):
+        B = lambda n: T[n + x]
+        op("v", [tok_i[x]], lambda: ts(B("KEY")[:, 0:1], B("MI")[:], 128.0, T.PC[:, 0:1], A.mult, A.add))
+        dk = op("v", [], lambda: ts(B("DK")[:], T.PM[:], B("KEY")[:, 0:1], None, A.mult))
+        st["R" + x] = op("t", [dk], lambda: g.tensor.matmul(B("RB")[:, 0:128], T.ONES[:], B("DK")[:], True, True))
+        op("v", [], lambda: ts(B("OI")[:], B("MI")[:], 12, None, A.logical_shift_right))
+        op("v", [], lambda: ts(B("KEY")[:, 2:3], B("OI")[:], 524288.0, 524287.0, A.mult, A.add))
+        op("v", [], lambda: ts(B("KEY")[:, 1:2], B("MI")[:], 128.0, 127.0, A.mult, A.add))
+        op("v", [], lambda: ts(B("LI")[:], B("MI")[:], RR - 1, None, A.bitwise_and))
+        op("v", [], lambda: ts(B("C0")[:, 0:1], B("OI")[:], float(W), float(-W * rb), A.mult, A.add))
+        op("v", [], lambda: ts(B("C0")[:, 2:3], B("LI")[:], float(-RR), None, A.add))
+        c0 = op("v", [], lambda: ts(B("C0")[:, 4:5], B("OI")[:], float(-rb), None, A.add))
+        op("t", [c0], lambda: g.tensor.matmul(B("SS")[:, 0:5], T.PM[:], B("C0")[:, 0:5], True, False))
+
+    def transpose(x):
+        B = lambda n: T[n + x]
+        return op("t", [tok_g[x], vconst], lambda: g.tensor.matmul(B("GP")[:, 0:128], B("G")[:], T.IDN[:], True, True))
+
+    def stage2(x):
+        B = lambda n: T[n + x]
+        for k, col in ((0, 2), (1, 1), (2, 0)):
+            a = op("v", [st["R" + x]], lambda: ts(B("AA")[:, 128 * k:128 * k + 128], B("RB")[:, 0:128],
+                                                  B("KEY")[:, col:col + 1], None, A.is_gt))
+            st["S" + x] = op("t", [a, vconst], lambda: g.tensor.matmul(
+                B("SS")[:, 0:5], B("AA")[:, 128 * k:128 * k + 128], T.KC[:, 5 * k:5 * k + 5], False, k == 2))
+
+    def stage3(x):
+        B = lambda n: T[n + x]
+        S = B("SS")
+        sel = op("v", [st["S" + x], gall], lambda: ts(B("SEL")[:], T.IOT[:], S[:, 0:1], None, A.is_equal))
+        op("t", [sel, st["GT" + x]], lambda: g.tensor.matmul(B("PK")[:, 0:NS], B("GT")[:], B("SEL")[:], True, False))
+        op("v", [], lambda: ts(B("VV")[:], S[:, 3:4], 0.0, S[:, 2:3], A.is_equal, A.mult))
+        op("v", [], lambda: ts(B("RM")[:], T.IOT[:, 0:8], S[:, 4:5], B("VV")[:, 0:1], A.is_equal, A.mult))
+        ll = op("v", [], lambda: ts(B("LL")[:], T.PAT[:], S[:, 1:2], None, A.is_equal))
+        for h in (0, 1):
+            st["P" + x] = op("t", [ll], lambda: g.tensor.matmul(
+                B("PK")[:, 32 + h:NS:W], B("LL")[:, 128 * h:128 * h + 128], B("RM")[:], False, h == 1))
+
+    def stage4(x):
+        B = lambda n: T[n + x]
+        st["PAY" + x] = op("v", [st["P" + x]], lambda: V.tensor_tensor(B("PAY")[:], B("PK")[:, 0:NS], T.TR[:], A.add))
+
+    def batch(x):
+        wait("g", st["PAY" + x])
+        base = 0 if x == "a" else 8
+        for k in range(0 if core != home else 1, 8):
+            b = (a_me + k) % 8
+            s = base + a_me
+            send(cores[rb + b], T.LAND[:, W * s:W * s + W], T["PAY" + x][:, W * b:W * b + W], "arr%d" % s)
+
+    if "a" in sets:
+        stage1("a")
+        tpa = transpose("a")
+        stage2("a")
+        st["GTa"] = op("v", [tpa], lambda: V.tensor_copy(T.GTa[:], T.GPa[:, 0:128]))
+        stage3("a")
+    if "b" in sets:
+        stage1("b")
+    if "a" in sets:
+        stage4("a")
+        batch("a")
+    if "b" in sets:
+        stage2("b")
+        tpb = transpose("b")
+        st["GTb"] = op("s", [tpb], lambda: g.scalar.activation(T.GTb[:], T.GPb[:, 0:128], ActivationFunctionType.Copy))
+        stage3("b")
+        stage4("b")
+        batch("b")
+
+    if rank is not None:
+        win = T.Y[:, 0:YW]
+        nround = [0]
+
+        def rnd(D, Fo, deps):
+            l = nround[0]
+            nround[0] += 1
+            off = T.OFFU[:, 2 * l:2 * l + 2]
+            op("v", deps, lambda: V.tensor_copy(off, Fo))
+            if l == 0:
+                return op("v", [zero], lambda: V.tensor_copy(win.indirect(off), D))
+            op("v", [], lambda: V.tensor_tensor(T.TMP[:], win.indirect(off), D, A.add))
+            return op("v", [], lambda: V.tensor_copy(win.indirect(off), T.TMP[:]))
+
+        last = None
+        for x, base in (("a", 0), ("b", 8)):
+            if x in sets:
+                c = W * a_me
+                last = rnd(T["PAY" + x][:, c:c + 32], T["PAY" + x][:, c + 32:c + W], [])
+            for k in range(1 if x in sets else 0, 8):
+                s = base + (a_me - k) % 8
+                src = cores[rb + (a_me - k) % 8] if x == "a" else worker[rb + (a_me - k) % 8]
+                tok = expect("arr%d" % s, neng(src, core))
+                last = rnd(T.LAND[:, W * s:W * s + 32], T.LAND[:, W * s + 32:W * s + W], [tok])
+        wait("y", last)
+        g.sync.dma_start(T.y[:], T.Y[:, 0:RR]).then_inc(T.sem.sty, 16)
+        expect("sty", 16)
+
+    for name in sorted(cnt):
+        wait("g", (name, cnt[name]))

@@ -1,6 +1,7 @@
+from concourse.bass import DstId, RemoteDMATransfer
 from concourse.mybir import dt, AluOpType, AxisListType, ActivationFunctionType
 
-HELP = False
+HELP = True
 W = 34
 NS = 8 * W
 RR = 4096
@@ -64,24 +65,31 @@ def rank_program(g, core, T, topo):
             Q[q].wait_ge(T.sem[name], val)
             seen[(q, name)] = val
 
-    def op(q, deps, fn):
+    def op(q, deps, fn, bar=False):
         own = OWN[q]
         for d in deps:
             wait(q, d)
-        if cnt.get(own, 0):
+        if bar and cnt.get(own, 0):
             wait(q, (own, cnt[own]))
         fn().then_inc(T.sem[own], 1)
         cnt[own] = cnt.get(own, 0) + 1
         return (own, cnt[own])
 
-    def neng(src, dst):
-        return bin(topo.mask(src, dst)).count("1")
+    def pop(m):
+        return bin(m).count("1")
 
     def send(dst, out_ap, in_ap, rsem):
         rid, pid = topo.addr(dst, core)
         g.remote_dma(out_ap=out_ap, in_ap=in_ap, remote_sem=T.sem[rsem], local_sem=T.sem.sent, pid=pid,
                      routing_id=rid, dma_engine_mask=topo.mask(core, dst))
-        cnt["sent"] = cnt.get("sent", 0) + neng(core, dst)
+        cnt["sent"] = cnt.get("sent", 0) + pop(topo.mask(core, dst))
+
+    def part_mask(src, a_src, b):
+        k = (b - a_src) % 8
+        if k == 0:
+            return topo.mask(src, cores[rb + b]) & ~topo.mask(src, cores[rb + (b + 1) % 8])
+        m = topo.mask(src, cores[rb + b])
+        return [1 << i for i in range(16) if (m >> i) & 1][k - 1]
 
     def expect(name, n):
         cnt[name] = cnt.get(name, 0) + n
@@ -89,6 +97,8 @@ def rank_program(g, core, T, topo):
 
     V = g.vector
     ts = V.tensor_scalar
+    mm = g.tensor.matmul
+    cp = ActivationFunctionType.Copy
     sets = ("a" if rank is not None else "") + ("b" if wrank is not None else "")
 
     tok_i = {}
@@ -99,41 +109,34 @@ def rank_program(g, core, T, topo):
         tok_i["a"] = expect("ldi", 16)
         tok_g["a"] = expect("ldg", 16)
     if wrank is not None:
-        tok_i["b"] = expect("rawi", neng(cores[partner], core))
-        tok_g["b"] = expect("rawg", neng(cores[partner], core))
+        tok_i["b"] = expect("rawi", pop(topo.mask(cores[partner], core)))
+        tok_g["b"] = expect("rawg", pop(topo.mask(cores[partner], core)))
 
     op("g", [], lambda: g.iota(T.PC[:], [[0, 1]], 0, 1, allow_small_or_imprecise_dtypes=True))
-    gq = op("g", [], lambda: g.iota(T.QROW[:], [[1, 8], [8, 16]], 0, 0, allow_small_or_imprecise_dtypes=True))
-    gio = op("g", [], lambda: g.iota(T.IOT[:], [[1, NS]], 0, 0, allow_small_or_imprecise_dtypes=True))
+    op("g", [], lambda: g.iota(T.QROW[:], [[1, 8], [8, 16]], 0, 0, allow_small_or_imprecise_dtypes=True))
+    op("g", [], lambda: g.iota(T.IOT[:], [[1, NS]], 0, 0, allow_small_or_imprecise_dtypes=True))
     op("g", [], lambda: g.iota(T.PAT[:], [[16, 2], [0, 8], [1, 16]], 0, 0, allow_small_or_imprecise_dtypes=True))
     gall = op("g", [], lambda: g.iota(T.PI[:], [[0, 1]], 0, 1))
 
     op("v", [], lambda: V.memset(T.ONES[:], 1.0))
-    op("v", [gq], lambda: ts(T.PM[:], T.QROW[:], T.PC[:, 0:1], None, A.is_equal))
     for x in sets:
         op("v", [], lambda: V.memset(T["C0" + x][:], 0.0))
-    op("v", [gio], lambda: ts(T.IDN[:], T.IOT[:, 0:128], T.PC[:, 0:1], None, A.is_equal))
-    op("v", [], lambda: V.memset(T.KC[:], 0.0))
-    op("v", [], lambda: V.memset(T.KC[:, 0:2], -1.0))
-    op("v", [], lambda: V.memset(T.KC[:, 2:3], 1.0))
-    op("v", [], lambda: V.memset(T.KC[:, 5:7], 1.0))
-    op("v", [], lambda: V.memset(T.KC[:, 7:9], -1.0))
-    op("v", [], lambda: V.memset(T.KC[:, 13:14], 1.0))
+    for lo, hi, val in ((0, 2, -1.0), (2, 3, 1.0), (3, 5, 0.0), (5, 7, 1.0), (7, 9, -1.0), (9, 13, 0.0), (13, 14, 1.0),
+                        (14, 16, 0.0)):
+        op("v", [], lambda: V.memset(T.KC[:, lo:hi], val))
     op("v", [], lambda: V.memset(T.TR[:], 0.0))
-    op("v", [gall], lambda: ts(T.P16I[:], T.PI[:], 15, None, A.bitwise_and))
-    op("v", [], lambda: ts(T.P16F[:, 0:1], T.P16I[:], float(RR), None, A.add))
-    op("v", [], lambda: ts(T.P16F[:, 1:2], T.P16I[:], float(RR + 16), None, A.add))
-    op("v", [], lambda: ts(T.TR[:, 32:NS:W], T.IOT[:, 0:8], 0.0, T.P16F[:, 0:1], A.mult, A.add))
-    vconst = op("v", [], lambda: ts(T.TR[:, 33:NS:W], T.IOT[:, 0:8], 0.0, T.P16F[:, 1:2], A.mult, A.add))
+    op("v", [gall], lambda: ts(T.PM[:], T.QROW[:], T.PC[:, 0:1], None, A.is_equal))
+    op("v", [], lambda: ts(T.IDN[:], T.IOT[:, 0:128], T.PC[:, 0:1], None, A.is_equal))
+    op("v", [], lambda: ts(T.P16I[:], T.PI[:], 15, None, A.bitwise_and))
+    todo = [2]
 
     zero = None
     if rank is not None:
-        cp = ActivationFunctionType.Copy
-        op("s", [gio], lambda: g.scalar.activation(T.Y[:, 0:NS], T.IOT[:], cp, scale=0.0))
+        op("s", [gall], lambda: g.scalar.activation(T.Y[:, 0:NS], T.IOT[:], cp, scale=0.0))
         have = NS
         while have < YW:
             n = min(have, YW - have)
-            zero = op("s", [], lambda: g.scalar.activation(T.Y[:, have:have + n], T.Y[:, 0:n], cp))
+            zero = op("s", [], lambda: g.scalar.activation(T.Y[:, have:have + n], T.Y[:, 0:n], cp), bar=True)
             have += n
 
     if rank is not None:
@@ -147,97 +150,110 @@ def rank_program(g, core, T, topo):
 
     def stage1(x):
         B = lambda n: T[n + x]
-        op("v", [tok_i[x]], lambda: ts(B("KEY")[:, 0:1], B("MI")[:], 128.0, T.PC[:, 0:1], A.mult, A.add))
-        dk = op("v", [], lambda: ts(B("DK")[:], T.PM[:], B("KEY")[:, 0:1], None, A.mult))
-        st["R" + x] = op("t", [dk], lambda: g.tensor.matmul(B("RB")[:, 0:128], T.ONES[:], B("DK")[:], True, True))
+        first = todo[0] == 2
+        todo[0] = 0
+        if first:
+            op("v", [], lambda: ts(T.P16F[:, 0:1], T.P16I[:], float(RR), None, A.add), bar=True)
+            op("v", [], lambda: ts(T.P16F[:, 1:2], T.P16I[:], float(RR + 16), None, A.add))
+        op("v", [tok_i[x]], lambda: ts(B("KEY")[:, 0:1], B("MI")[:], 128.0, T.PC[:, 0:1], A.mult, A.add), bar=not first)
         op("v", [], lambda: ts(B("OI")[:], B("MI")[:], 12, None, A.logical_shift_right))
-        op("v", [], lambda: ts(B("KEY")[:, 2:3], B("OI")[:], 524288.0, 524287.0, A.mult, A.add))
         op("v", [], lambda: ts(B("KEY")[:, 1:2], B("MI")[:], 128.0, 127.0, A.mult, A.add))
         op("v", [], lambda: ts(B("LI")[:], B("MI")[:], RR - 1, None, A.bitwise_and))
+        op("v", [], lambda: ts(B("DK")[:], T.PM[:], B("KEY")[:, 0:1], None, A.mult), bar=True)
+        op("v", [], lambda: ts(B("KEY")[:, 2:3], B("OI")[:], 524288.0, 524287.0, A.mult, A.add))
         op("v", [], lambda: ts(B("C0")[:, 0:1], B("OI")[:], float(W), float(-W * rb), A.mult, A.add))
         op("v", [], lambda: ts(B("C0")[:, 2:3], B("LI")[:], float(-RR), None, A.add))
-        c0 = op("v", [], lambda: ts(B("C0")[:, 4:5], B("OI")[:], float(-rb), None, A.add))
-        op("t", [c0], lambda: g.tensor.matmul(B("SS")[:, 0:5], T.PM[:], B("C0")[:, 0:5], True, False))
-
-    def transpose(x):
-        B = lambda n: T[n + x]
-        return op("t", [tok_g[x], vconst], lambda: g.tensor.matmul(B("GP")[:, 0:128], B("G")[:], T.IDN[:], True, True))
+        g2 = op("v", [], lambda: ts(B("C0")[:, 4:5], B("OI")[:], float(-rb), None, A.add))
+        if first:
+            op("v", [], lambda: ts(T.TR[:, 32:NS:W], T.IOT[:, 0:8], 0.0, T.P16F[:, 0:1], A.mult, A.add))
+            g2 = op("v", [], lambda: ts(T.TR[:, 33:NS:W], T.IOT[:, 0:8], 0.0, T.P16F[:, 1:2], A.mult, A.add))
+        r = op("t", [g2], lambda: mm(B("RB")[:, 0:128], T.ONES[:], B("DK")[:], True, True), bar=True)
+        op("t", [], lambda: mm(B("SS")[:, 0:5], T.PM[:], B("C0")[:, 0:5], True, False), bar=True)
+        st["R" + x] = r
 
     def stage2(x):
         B = lambda n: T[n + x]
+        a = None
         for k, col in ((0, 2), (1, 1), (2, 0)):
             a = op("v", [st["R" + x]], lambda: ts(B("AA")[:, 128 * k:128 * k + 128], B("RB")[:, 0:128],
-                                                  B("KEY")[:, col:col + 1], None, A.is_gt))
-            st["S" + x] = op("t", [a, vconst], lambda: g.tensor.matmul(
-                B("SS")[:, 0:5], B("AA")[:, 128 * k:128 * k + 128], T.KC[:, 5 * k:5 * k + 5], False, k == 2))
+                                                  B("KEY")[:, col:col + 1], None, A.is_gt), bar=(k == 0))
+        for k in range(3):
+            op("t", [a], lambda: mm(B("SS")[:, 0:5], B("AA")[:, 128 * k:128 * k + 128], T.KC[:, 5 * k:5 * k + 5],
+                                    False, k == 2))
+        st["S" + x] = op("t", [tok_g[x]], lambda: mm(B("GP")[:, 0:128], B("G")[:], T.IDN[:], True, True))
 
-    def stage3(x):
+    def stage3(x, evq):
         B = lambda n: T[n + x]
         S = B("SS")
-        sel = op("v", [st["S" + x], gall], lambda: ts(B("SEL")[:], T.IOT[:], S[:, 0:1], None, A.is_equal))
-        op("t", [sel, st["GT" + x]], lambda: g.tensor.matmul(B("PK")[:, 0:NS], B("GT")[:], B("SEL")[:], True, False))
-        op("v", [], lambda: ts(B("VV")[:], S[:, 3:4], 0.0, S[:, 2:3], A.is_equal, A.mult))
-        op("v", [], lambda: ts(B("RM")[:], T.IOT[:, 0:8], S[:, 4:5], B("VV")[:, 0:1], A.is_equal, A.mult))
-        ll = op("v", [], lambda: ts(B("LL")[:], T.PAT[:], S[:, 1:2], None, A.is_equal))
+        gt = None
+        if evq == "s":
+            gt = op("s", [st["S" + x]], lambda: g.scalar.activation(B("GT")[:], B("GP")[:, 0:128], cp), bar=True)
+        op("v", [st["S" + x]], lambda: ts(B("SEL")[:], T.IOT[:], S[:, 0:1], None, A.is_equal), bar=True)
+        if evq == "v":
+            op("v", [], lambda: V.tensor_copy(B("GT")[:], B("GP")[:, 0:128]))
+        g4 = op("v", [], lambda: ts(B("VV")[:], S[:, 3:4], 0.0, S[:, 2:3], A.is_equal, A.mult))
+        op("t", [g4, gt], lambda: mm(B("PK")[:, 0:NS], B("GT")[:], B("SEL")[:], True, False), bar=True)
+        op("v", [], lambda: ts(B("RM")[:], T.IOT[:, 0:8], S[:, 4:5], B("VV")[:, 0:1], A.is_equal, A.mult), bar=True)
+        g5 = op("v", [], lambda: ts(B("LL")[:], T.PAT[:], S[:, 1:2], None, A.is_equal))
         for h in (0, 1):
-            st["P" + x] = op("t", [ll], lambda: g.tensor.matmul(
-                B("PK")[:, 32 + h:NS:W], B("LL")[:, 128 * h:128 * h + 128], B("RM")[:], False, h == 1))
+            st["P" + x] = op("t", [g5], lambda: mm(B("PK")[:, 32 + h:NS:W], B("LL")[:, 128 * h:128 * h + 128],
+                                                   B("RM")[:], False, h == 1))
 
     def stage4(x):
         B = lambda n: T[n + x]
-        st["PAY" + x] = op("v", [st["P" + x]], lambda: V.tensor_tensor(B("PAY")[:], B("PK")[:, 0:NS], T.TR[:], A.add))
+        st["PAY" + x] = op("v", [st["P" + x]], lambda: V.tensor_tensor(B("PAY")[:], B("PK")[:, 0:NS], T.TR[:], A.add),
+                           bar=True)
 
     def batch(x):
         wait("g", st["PAY" + x])
-        base = 0 if x == "a" else 8
+        s = (0 if x == "a" else 8) + a_me
+        trs = []
         for k in range(0 if core != home else 1, 8):
             b = (a_me + k) % 8
-            s = base + a_me
-            send(cores[rb + b], T.LAND[:, W * s:W * s + W], T["PAY" + x][:, W * b:W * b + W], "arr%d" % s)
+            rid, pid = topo.addr(cores[rb + b], core)
+            m = part_mask(core, a_me, b)
+            trs.append(RemoteDMATransfer(dst_ids=[DstId(rid=rid, pnc=pid)], dma_engine_mask=m,
+                                         remote_sem=T.sem["arr%d" % s], src=T["PAY" + x][:, W * b:W * b + W],
+                                         dst=T.LAND[:, W * s:W * s + W]))
+            cnt["sent"] = cnt.get("sent", 0) + pop(m)
+        g.remote_dma_fused(trs, local_sem=T.sem.sent)
 
-    if "a" in sets:
-        stage1("a")
-        tpa = transpose("a")
-        stage2("a")
-        st["GTa"] = op("v", [tpa], lambda: V.tensor_copy(T.GTa[:], T.GPa[:, 0:128]))
-        stage3("a")
-    if "b" in sets:
-        stage1("b")
-    if "a" in sets:
-        stage4("a")
-        batch("a")
-    if "b" in sets:
-        stage2("b")
-        tpb = transpose("b")
-        st["GTb"] = op("s", [tpb], lambda: g.scalar.activation(T.GTb[:], T.GPb[:, 0:128], ActivationFunctionType.Copy))
-        stage3("b")
-        stage4("b")
-        batch("b")
+    for x in sets:
+        stage1(x)
+        stage2(x)
+        stage3(x, "v" if rank is not None else "s")
+        stage4(x)
+        batch(x)
 
     if rank is not None:
         win = T.Y[:, 0:YW]
-        nround = [0]
-
-        def rnd(D, Fo, deps):
-            l = nround[0]
-            nround[0] += 1
-            off = T.OFFU[:, 2 * l:2 * l + 2]
-            op("v", deps, lambda: V.tensor_copy(off, Fo))
-            if l == 0:
-                return op("v", [zero], lambda: V.tensor_copy(win.indirect(off), D))
-            op("v", [], lambda: V.tensor_tensor(T.TMP[:], win.indirect(off), D, A.add))
-            return op("v", [], lambda: V.tensor_copy(win.indirect(off), T.TMP[:]))
-
-        last = None
+        parts = []
         for x, base in (("a", 0), ("b", 8)):
+            lst = []
             if x in sets:
                 c = W * a_me
-                last = rnd(T["PAY" + x][:, c:c + 32], T["PAY" + x][:, c + 32:c + W], [])
+                lst.append((T["PAY" + x][:, c:c + 32], T["PAY" + x][:, c + 32:c + W], None))
             for k in range(1 if x in sets else 0, 8):
-                s = base + (a_me - k) % 8
-                src = cores[rb + (a_me - k) % 8] if x == "a" else worker[rb + (a_me - k) % 8]
-                tok = expect("arr%d" % s, neng(src, core))
-                last = rnd(T.LAND[:, W * s:W * s + 32], T.LAND[:, W * s + 32:W * s + W], [tok])
+                a_src = (a_me - k) % 8
+                s = base + a_src
+                src = cores[rb + a_src] if x == "a" else worker[rb + a_src]
+                tok = expect("arr%d" % s, pop(part_mask(src, a_src, a_me)))
+                lst.append((T.LAND[:, W * s:W * s + 32], T.LAND[:, W * s + 32:W * s + W], tok))
+            parts.append(lst)
+        last = None
+        l = 0
+        for lst in parts:
+            for i, (D, Fo, tok) in enumerate(lst):
+                off = T.OFFU[:, 2 * (l + i):2 * (l + i) + 2]
+                op("v", [tok], lambda: V.tensor_copy(off, Fo), bar=(l == 0 and i == 0))
+            for D, Fo, tok in lst:
+                off = T.OFFU[:, 2 * l:2 * l + 2]
+                if l == 0:
+                    last = op("v", [zero], lambda: V.tensor_copy(win.indirect(off), D), bar=True)
+                else:
+                    op("v", [], lambda: V.tensor_tensor(T.TMP[:], win.indirect(off), D, A.add), bar=True)
+                    last = op("v", [], lambda: V.tensor_copy(win.indirect(off), T.TMP[:]), bar=True)
+                l += 1
         wait("y", last)
         g.sync.dma_start(T.y[:], T.Y[:, 0:RR]).then_inc(T.sem.sty, 16)
         expect("sty", 16)

@@ -6,6 +6,7 @@ W = 34
 NS = 8 * W
 RR = 4096
 YW = RR + 32
+CALLS = ((0, 1, 2), (3, 4), (5, 6), (7,))
 
 F, I32, BF = "float32", "int32", "bfloat16"
 SCRATCH = {
@@ -89,7 +90,11 @@ def rank_program(g, core, T, topo):
         if k == 0:
             return topo.mask(src, cores[rb + b]) & ~topo.mask(src, cores[rb + (b + 1) % 8])
         m = topo.mask(src, cores[rb + b])
-        return [1 << i for i in range(16) if (m >> i) & 1][k - 1]
+        if k == 7:
+            return m
+        bits = [1 << i for i in range(16) if (m >> i) & 1]
+        h = len(bits) // 2
+        return sum(bits[h * ((k - 1) % 2):h * ((k - 1) % 2) + h])
 
     def expect(name, n):
         cnt[name] = cnt.get(name, 0) + n
@@ -207,16 +212,19 @@ def rank_program(g, core, T, topo):
     def batch(x):
         wait("g", st["PAY" + x])
         s = (0 if x == "a" else 8) + a_me
-        trs = []
-        for k in range(0 if core != home else 1, 8):
-            b = (a_me + k) % 8
-            rid, pid = topo.addr(cores[rb + b], core)
-            m = part_mask(core, a_me, b)
-            trs.append(RemoteDMATransfer(dst_ids=[DstId(rid=rid, pnc=pid)], dma_engine_mask=m,
-                                         remote_sem=T.sem["arr%d" % s], src=T["PAY" + x][:, W * b:W * b + W],
-                                         dst=T.LAND[:, W * s:W * s + W]))
-            cnt["sent"] = cnt.get("sent", 0) + pop(m)
-        g.remote_dma_fused(trs, local_sem=T.sem.sent)
+        for ks in CALLS:
+            trs = []
+            for k in ks:
+                if k == 0 and core == home:
+                    continue
+                b = (a_me + k) % 8
+                rid, pid = topo.addr(cores[rb + b], core)
+                m = part_mask(core, a_me, b)
+                trs.append(RemoteDMATransfer(dst_ids=[DstId(rid=rid, pnc=pid)], dma_engine_mask=m,
+                                             remote_sem=T.sem["arr%d" % s], src=T["PAY" + x][:, W * b:W * b + W],
+                                             dst=T.LAND[:, W * s:W * s + W]))
+                cnt["sent"] = cnt.get("sent", 0) + pop(m)
+            g.remote_dma_fused(trs, local_sem=T.sem.sent)
 
     for x in sets:
         stage1(x)
@@ -229,17 +237,19 @@ def rank_program(g, core, T, topo):
         win = T.Y[:, 0:YW]
         parts = []
         for x, base in (("a", 0), ("b", 8)):
-            lst = []
-            if x in sets:
-                c = W * a_me
-                lst.append((T["PAY" + x][:, c:c + 32], T["PAY" + x][:, c + 32:c + W], None))
-            for k in range(1 if x in sets else 0, 8):
-                a_src = (a_me - k) % 8
-                s = base + a_src
-                src = cores[rb + a_src] if x == "a" else worker[rb + a_src]
-                tok = expect("arr%d" % s, pop(part_mask(src, a_src, a_me)))
-                lst.append((T.LAND[:, W * s:W * s + 32], T.LAND[:, W * s + 32:W * s + W], tok))
-            parts.append(lst)
+            for ks in CALLS:
+                lst = []
+                for k in ks:
+                    a_src = (a_me - k) % 8
+                    s = base + a_src
+                    if k == 0 and x in sets:
+                        c = W * a_me
+                        lst.append((T["PAY" + x][:, c:c + 32], T["PAY" + x][:, c + 32:c + W], None))
+                        continue
+                    src = cores[rb + a_src] if x == "a" else worker[rb + a_src]
+                    tok = expect("arr%d" % s, pop(part_mask(src, a_src, a_me)))
+                    lst.append((T.LAND[:, W * s:W * s + 32], T.LAND[:, W * s + 32:W * s + W], tok))
+                parts.append(lst)
         last = None
         l = 0
         for lst in parts:

@@ -6,7 +6,7 @@ W = 34
 NS = 8 * W
 RR = 4096
 YW = RR + 32
-CALLS = ((0, 1, 2), (3, 4), (5, 6), (7,))
+CALLS = {"a": ((0,), (1, 2), (3, 4), (5, 6), (7,)), "b": ((1, 2), (3, 4, 0), (5, 6), (7,))}
 
 F, I32, BF = "float32", "int32", "bfloat16"
 SCRATCH = {
@@ -27,7 +27,7 @@ for _x in "ab":
         "RB" + _x: ("psum", [128, 512], F), "SS" + _x: ("psum", [128, 512], F),
         "GP" + _x: ("psum", [128, 512], F), "PK" + _x: ("psum", [128, 512], F),
     })
-SEMAPHORES = ["v", "t", "s", "gi", "ldi", "ldg", "sty", "sent", "rawi", "rawg"] + ["arr%d" % k for k in range(16)]
+SEMAPHORES = ["v", "t", "s", "gi", "z", "ldi", "ldg", "sty", "sent", "rawi", "rawg"] + ["arr%d" % k for k in range(16)]
 
 
 def _helper(topo, c):
@@ -105,6 +105,7 @@ def rank_program(g, core, T, topo):
     mm = g.tensor.matmul
     cp = ActivationFunctionType.Copy
     sets = ("a" if rank is not None else "") + ("b" if wrank is not None else "")
+    assert len(sets) == 1
 
     tok_i = {}
     tok_g = {}
@@ -117,11 +118,13 @@ def rank_program(g, core, T, topo):
         tok_i["b"] = expect("rawi", pop(topo.mask(cores[partner], core)))
         tok_g["b"] = expect("rawg", pop(topo.mask(cores[partner], core)))
 
+    ztok = None
+    if rank is not None:
+        V.memset(T.Y[:, 0:128], 0.0).then_inc(T.sem.z, 1)
+        ztok = expect("z", 1)
     op("g", [], lambda: g.iota(T.PC[:], [[0, 1]], 0, 1, allow_small_or_imprecise_dtypes=True))
     op("g", [], lambda: g.iota(T.QROW[:], [[1, 8], [8, 16]], 0, 0, allow_small_or_imprecise_dtypes=True))
-    op("g", [], lambda: g.iota(T.IOT[:], [[1, NS]], 0, 0, allow_small_or_imprecise_dtypes=True))
-    op("g", [], lambda: g.iota(T.PAT[:], [[16, 2], [0, 8], [1, 16]], 0, 0, allow_small_or_imprecise_dtypes=True))
-    gall = op("g", [], lambda: g.iota(T.PI[:], [[0, 1]], 0, 1))
+    g1c = op("g", [], lambda: g.iota(T.IOT[:, 0:128], [[1, 128]], 0, 0, allow_small_or_imprecise_dtypes=True))
 
     op("v", [], lambda: V.memset(T.ONES[:], 1.0))
     for x in sets:
@@ -130,37 +133,34 @@ def rank_program(g, core, T, topo):
                         (14, 16, 0.0)):
         op("v", [], lambda: V.memset(T.KC[:, lo:hi], val))
     op("v", [], lambda: V.memset(T.TR[:], 0.0))
-    op("v", [gall], lambda: ts(T.PM[:], T.QROW[:], T.PC[:, 0:1], None, A.is_equal))
+    op("v", [g1c], lambda: ts(T.PM[:], T.QROW[:], T.PC[:, 0:1], None, A.is_equal))
     op("v", [], lambda: ts(T.IDN[:], T.IOT[:, 0:128], T.PC[:, 0:1], None, A.is_equal))
-    op("v", [], lambda: ts(T.P16I[:], T.PI[:], 15, None, A.bitwise_and))
-    todo = [2]
 
     zero = None
     if rank is not None:
-        op("s", [gall], lambda: g.scalar.activation(T.Y[:, 0:NS], T.IOT[:], cp, scale=0.0))
-        have = NS
+        have = 128
         while have < YW:
             n = min(have, YW - have)
-            zero = op("s", [], lambda: g.scalar.activation(T.Y[:, have:have + n], T.Y[:, 0:n], cp), bar=True)
+            zero = op("s", [ztok], lambda: g.scalar.activation(T.Y[:, have:have + n], T.Y[:, 0:n], cp), bar=True)
             have += n
 
+    dst = worker[partner]
     if rank is not None:
-        dst = worker[partner]
         wait("g", tok_i["a"])
         send(dst, T.MIb[:], T.MIa[:], "rawi")
+    op("g", [], lambda: g.iota(T.IOT[:, 128:NS], [[1, NS - 128]], 128, 0, allow_small_or_imprecise_dtypes=True), bar=True)
+    g2c = op("g", [], lambda: g.iota(T.PI[:], [[0, 1]], 0, 1))
+    if rank is not None:
         wait("g", tok_g["a"])
         send(dst, T.Gb[:], T.Ga[:], "rawg")
+    g3c = op("g", [], lambda: g.iota(T.PAT[:], [[16, 2], [0, 8], [1, 16]], 0, 0, allow_small_or_imprecise_dtypes=True),
+             bar=True)
 
     st = {}
 
     def stage1(x):
         B = lambda n: T[n + x]
-        first = todo[0] == 2
-        todo[0] = 0
-        if first:
-            op("v", [], lambda: ts(T.P16F[:, 0:1], T.P16I[:], float(RR), None, A.add), bar=True)
-            op("v", [], lambda: ts(T.P16F[:, 1:2], T.P16I[:], float(RR + 16), None, A.add))
-        op("v", [tok_i[x]], lambda: ts(B("KEY")[:, 0:1], B("MI")[:], 128.0, T.PC[:, 0:1], A.mult, A.add), bar=not first)
+        op("v", [tok_i[x]], lambda: ts(B("KEY")[:, 0:1], B("MI")[:], 128.0, T.PC[:, 0:1], A.mult, A.add), bar=True)
         op("v", [], lambda: ts(B("OI")[:], B("MI")[:], 12, None, A.logical_shift_right))
         op("v", [], lambda: ts(B("KEY")[:, 1:2], B("MI")[:], 128.0, 127.0, A.mult, A.add))
         op("v", [], lambda: ts(B("LI")[:], B("MI")[:], RR - 1, None, A.bitwise_and))
@@ -169,23 +169,21 @@ def rank_program(g, core, T, topo):
         op("v", [], lambda: ts(B("C0")[:, 0:1], B("OI")[:], float(W), float(-W * rb), A.mult, A.add))
         op("v", [], lambda: ts(B("C0")[:, 2:3], B("LI")[:], float(-RR), None, A.add))
         g2 = op("v", [], lambda: ts(B("C0")[:, 4:5], B("OI")[:], float(-rb), None, A.add))
-        if first:
-            op("v", [], lambda: ts(T.TR[:, 32:NS:W], T.IOT[:, 0:8], 0.0, T.P16F[:, 0:1], A.mult, A.add))
-            g2 = op("v", [], lambda: ts(T.TR[:, 33:NS:W], T.IOT[:, 0:8], 0.0, T.P16F[:, 1:2], A.mult, A.add))
         r = op("t", [g2], lambda: mm(B("RB")[:, 0:128], T.ONES[:], B("DK")[:], True, True), bar=True)
         op("t", [], lambda: mm(B("SS")[:, 0:5], T.PM[:], B("C0")[:, 0:5], True, False), bar=True)
+        op("t", [tok_g[x]], lambda: mm(B("GP")[:, 0:128], B("G")[:], T.IDN[:], True, True))
         st["R" + x] = r
 
     def stage2(x):
         B = lambda n: T[n + x]
+        op("v", [g2c], lambda: ts(T.P16I[:], T.PI[:], 15, None, A.bitwise_and), bar=True)
         a = None
         for k, col in ((0, 2), (1, 1), (2, 0)):
             a = op("v", [st["R" + x]], lambda: ts(B("AA")[:, 128 * k:128 * k + 128], B("RB")[:, 0:128],
-                                                  B("KEY")[:, col:col + 1], None, A.is_gt), bar=(k == 0))
+                                                  B("KEY")[:, col:col + 1], None, A.is_gt))
         for k in range(3):
-            op("t", [a], lambda: mm(B("SS")[:, 0:5], B("AA")[:, 128 * k:128 * k + 128], T.KC[:, 5 * k:5 * k + 5],
-                                    False, k == 2))
-        st["S" + x] = op("t", [tok_g[x]], lambda: mm(B("GP")[:, 0:128], B("G")[:], T.IDN[:], True, True))
+            st["S" + x] = op("t", [a], lambda: mm(B("SS")[:, 0:5], B("AA")[:, 128 * k:128 * k + 128],
+                                                  T.KC[:, 5 * k:5 * k + 5], False, k == 2))
 
     def stage3(x, evq):
         B = lambda n: T[n + x]
@@ -199,10 +197,14 @@ def rank_program(g, core, T, topo):
         g4 = op("v", [], lambda: ts(B("VV")[:], S[:, 3:4], 0.0, S[:, 2:3], A.is_equal, A.mult))
         op("t", [g4, gt], lambda: mm(B("PK")[:, 0:NS], B("GT")[:], B("SEL")[:], True, False), bar=True)
         op("v", [], lambda: ts(B("RM")[:], T.IOT[:, 0:8], S[:, 4:5], B("VV")[:, 0:1], A.is_equal, A.mult), bar=True)
-        g5 = op("v", [], lambda: ts(B("LL")[:], T.PAT[:], S[:, 1:2], None, A.is_equal))
+        op("v", [], lambda: ts(T.P16F[:, 0:1], T.P16I[:], float(RR), None, A.add))
+        op("v", [], lambda: ts(T.P16F[:, 1:2], T.P16I[:], float(RR + 16), None, A.add))
+        g5 = op("v", [g3c], lambda: ts(B("LL")[:], T.PAT[:], S[:, 1:2], None, A.is_equal))
         for h in (0, 1):
             st["P" + x] = op("t", [g5], lambda: mm(B("PK")[:, 32 + h:NS:W], B("LL")[:, 128 * h:128 * h + 128],
                                                    B("RM")[:], False, h == 1))
+        op("v", [], lambda: ts(T.TR[:, 32:NS:W], T.IOT[:, 0:8], 0.0, T.P16F[:, 0:1], A.mult, A.add), bar=True)
+        op("v", [], lambda: ts(T.TR[:, 33:NS:W], T.IOT[:, 0:8], 0.0, T.P16F[:, 1:2], A.mult, A.add))
 
     def stage4(x):
         B = lambda n: T[n + x]
@@ -212,7 +214,7 @@ def rank_program(g, core, T, topo):
     def batch(x):
         wait("g", st["PAY" + x])
         s = (0 if x == "a" else 8) + a_me
-        for ks in CALLS:
+        for ks in CALLS[x]:
             trs = []
             for k in ks:
                 if k == 0 and core == home:
@@ -224,7 +226,8 @@ def rank_program(g, core, T, topo):
                                              remote_sem=T.sem["arr%d" % s], src=T["PAY" + x][:, W * b:W * b + W],
                                              dst=T.LAND[:, W * s:W * s + W]))
                 cnt["sent"] = cnt.get("sent", 0) + pop(m)
-            g.remote_dma_fused(trs, local_sem=T.sem.sent)
+            if trs:
+                g.remote_dma_fused(trs, local_sem=T.sem.sent)
 
     for x in sets:
         stage1(x)
@@ -237,7 +240,7 @@ def rank_program(g, core, T, topo):
         win = T.Y[:, 0:YW]
         parts = []
         for x, base in (("a", 0), ("b", 8)):
-            for ks in CALLS:
+            for ks in CALLS[x]:
                 lst = []
                 for k in ks:
                     a_src = (a_me - k) % 8

from concourse.bass import DstId, RemoteDMATransfer
from concourse.mybir import dt, AluOpType, AxisListType, ActivationFunctionType

HELP = True
W = 34
NS = 8 * W
RR = 4096
YW = RR + 32
CALLS = {"a": ((0,), (1, 2), (3, 4), (5, 6), (7,)), "b": ((1, 2), (3, 4, 0), (5, 6), (7,))}

F, I32, BF = "float32", "int32", "bfloat16"
SCRATCH = {
    "IOT": ("sbuf", [128, NS], F), "PC": ("sbuf", [128, 1], F), "QROW": ("sbuf", [128, 128], F),
    "PAT": ("sbuf", [128, 256], F), "PI": ("sbuf", [128, 1], I32), "P16I": ("sbuf", [128, 1], I32),
    "P16F": ("sbuf", [128, 2], F), "ONES": ("sbuf", [128, 128], F), "IDN": ("sbuf", [128, 128], F),
    "PM": ("sbuf", [128, 128], F), "KC": ("sbuf", [128, 16], BF), "TR": ("sbuf", [128, NS], F),
    "LAND": ("sbuf", [128, 16 * W], F), "OFFU": ("sbuf", [128, 32], "uint16"), "TMP": ("sbuf", [128, 32], F),
    "Y": ("sbuf", [128, YW], F),
}
for _x in "ab":
    SCRATCH.update({
        "MI" + _x: ("sbuf", [128, 1], I32), "G" + _x: ("sbuf", [128, 128], F), "OI" + _x: ("sbuf", [128, 1], I32),
        "LI" + _x: ("sbuf", [128, 1], I32), "KEY" + _x: ("sbuf", [128, 4], F), "C0" + _x: ("sbuf", [128, 8], F),
        "DK" + _x: ("sbuf", [128, 128], F), "AA" + _x: ("sbuf", [128, 384], BF), "SEL" + _x: ("sbuf", [128, NS], F),
        "LL" + _x: ("sbuf", [128, 256], F), "VV" + _x: ("sbuf", [128, 1], F), "RM" + _x: ("sbuf", [128, 8], F),
        "GT" + _x: ("sbuf", [128, 128], F), "PAY" + _x: ("sbuf", [128, NS], F),
        "RB" + _x: ("psum", [128, 512], F), "SS" + _x: ("psum", [128, 512], F),
        "GP" + _x: ("psum", [128, 512], F), "PK" + _x: ("psum", [128, 512], F),
    })
SEMAPHORES = ["v", "t", "s", "gi", "z", "ldi", "ldg", "sty", "sent", "rawi", "rawg"] + ["arr%d" % k for k in range(16)]


def _helper(topo, c):
    same = [x for x in range(max(0, c - 8), c + 9)
            if x != c and topo.host(x) == topo.host(c) and topo.chip(x) == topo.chip(c)]
    return [x for x in same if topo.die(x) != topo.die(c)][0]


def rank_program(g, core, T, topo):
    A = AluOpType
    cores = list(T.cores)
    worker = [(_helper(topo, c) if HELP else c) for c in cores]
    rank = T.rank_of(core)
    wrank = worker.index(core) if core in worker else None
    if rank is None and wrank is None:
        return
    me = rank if rank is not None else wrank
    home = cores[me]
    myrack = topo.rack(topo.host(home))
    mates = [i for i in range(len(cores)) if topo.rack(topo.host(cores[i])) == myrack]
    rb = mates[0]
    assert mates == list(range(rb, rb + 8))
    partner = [i for i in range(len(cores)) if i not in mates and topo.may_write(home, cores[i])
               and topo.chip(cores[i]) == topo.chip(home)][0]
    a_me = me - rb

    Q = {"v": g.vector, "t": g.tensor, "s": g.scalar, "g": g, "y": g.sync}
    OWN = {"v": "v", "t": "t", "s": "s", "g": "gi"}
    cnt, seen = {}, {}

    def wait(q, tok):
        if tok is None:
            return
        name, val = tok
        if seen.get((q, name), 0) < val:
            Q[q].wait_ge(T.sem[name], val)
            seen[(q, name)] = val

    def op(q, deps, fn, bar=False):
        own = OWN[q]
        for d in deps:
            wait(q, d)
        if bar and cnt.get(own, 0):
            wait(q, (own, cnt[own]))
        fn().then_inc(T.sem[own], 1)
        cnt[own] = cnt.get(own, 0) + 1
        return (own, cnt[own])

    def pop(m):
        return bin(m).count("1")

    def send(dst, out_ap, in_ap, rsem):
        rid, pid = topo.addr(dst, core)
        g.remote_dma(out_ap=out_ap, in_ap=in_ap, remote_sem=T.sem[rsem], local_sem=T.sem.sent, pid=pid,
                     routing_id=rid, dma_engine_mask=topo.mask(core, dst))
        cnt["sent"] = cnt.get("sent", 0) + pop(topo.mask(core, dst))

    def part_mask(src, a_src, b):
        k = (b - a_src) % 8
        if k == 0:
            return topo.mask(src, cores[rb + b]) & ~topo.mask(src, cores[rb + (b + 1) % 8])
        m = topo.mask(src, cores[rb + b])
        if k == 7:
            return m
        bits = [1 << i for i in range(16) if (m >> i) & 1]
        h = len(bits) // 2
        return sum(bits[h * ((k - 1) % 2):h * ((k - 1) % 2) + h])

    def expect(name, n):
        cnt[name] = cnt.get(name, 0) + n
        return (name, cnt[name])

    V = g.vector
    ts = V.tensor_scalar
    mm = g.tensor.matmul
    cp = ActivationFunctionType.Copy
    sets = ("a" if rank is not None else "") + ("b" if wrank is not None else "")
    assert len(sets) == 1

    tok_i = {}
    tok_g = {}
    if rank is not None:
        g.sync.dma_start(T.MIa[:, 0:1], T.idx[:]).then_inc(T.sem.ldi, 16)
        g.sync.dma_start(T.Ga[:], T.gr[:]).then_inc(T.sem.ldg, 16)
        tok_i["a"] = expect("ldi", 16)
        tok_g["a"] = expect("ldg", 16)
    if wrank is not None:
        tok_i["b"] = expect("rawi", pop(topo.mask(cores[partner], core)))
        tok_g["b"] = expect("rawg", pop(topo.mask(cores[partner], core)))

    ztok = None
    if rank is not None:
        V.memset(T.Y[:, 0:128], 0.0).then_inc(T.sem.z, 1)
        ztok = expect("z", 1)
    op("g", [], lambda: g.iota(T.PC[:], [[0, 1]], 0, 1, allow_small_or_imprecise_dtypes=True))
    op("g", [], lambda: g.iota(T.QROW[:], [[1, 8], [8, 16]], 0, 0, allow_small_or_imprecise_dtypes=True))
    g1c = op("g", [], lambda: g.iota(T.IOT[:, 0:128], [[1, 128]], 0, 0, allow_small_or_imprecise_dtypes=True))

    op("v", [], lambda: V.memset(T.ONES[:], 1.0))
    for x in sets:
        op("v", [], lambda: V.memset(T["C0" + x][:], 0.0))
    for lo, hi, val in ((0, 2, -1.0), (2, 3, 1.0), (3, 5, 0.0), (5, 7, 1.0), (7, 9, -1.0), (9, 13, 0.0), (13, 14, 1.0),
                        (14, 16, 0.0)):
        op("v", [], lambda: V.memset(T.KC[:, lo:hi], val))
    op("v", [], lambda: V.memset(T.TR[:], 0.0))
    op("v", [g1c], lambda: ts(T.PM[:], T.QROW[:], T.PC[:, 0:1], None, A.is_equal))
    op("v", [], lambda: ts(T.IDN[:], T.IOT[:, 0:128], T.PC[:, 0:1], None, A.is_equal))

    zero = None
    if rank is not None:
        have = 128
        while have < YW:
            n = min(have, YW - have)
            zero = op("s", [ztok], lambda: g.scalar.activation(T.Y[:, have:have + n], T.Y[:, 0:n], cp), bar=True)
            have += n

    dst = worker[partner]
    if rank is not None:
        wait("g", tok_i["a"])
        send(dst, T.MIb[:], T.MIa[:], "rawi")
    op("g", [], lambda: g.iota(T.IOT[:, 128:NS], [[1, NS - 128]], 128, 0, allow_small_or_imprecise_dtypes=True), bar=True)
    g2c = op("g", [], lambda: g.iota(T.PI[:], [[0, 1]], 0, 1))
    if rank is not None:
        wait("g", tok_g["a"])
        send(dst, T.Gb[:], T.Ga[:], "rawg")
    g3c = op("g", [], lambda: g.iota(T.PAT[:], [[16, 2], [0, 8], [1, 16]], 0, 0, allow_small_or_imprecise_dtypes=True),
             bar=True)

    st = {}

    def stage1(x):
        B = lambda n: T[n + x]
        op("v", [tok_i[x]], lambda: ts(B("KEY")[:, 0:1], B("MI")[:], 128.0, T.PC[:, 0:1], A.mult, A.add), bar=True)
        op("v", [], lambda: ts(B("OI")[:], B("MI")[:], 12, None, A.logical_shift_right))
        op("v", [], lambda: ts(B("KEY")[:, 1:2], B("MI")[:], 128.0, 127.0, A.mult, A.add))
        op("v", [], lambda: ts(B("LI")[:], B("MI")[:], RR - 1, None, A.bitwise_and))
        op("v", [], lambda: ts(B("DK")[:], T.PM[:], B("KEY")[:, 0:1], None, A.mult), bar=True)
        op("v", [], lambda: ts(B("KEY")[:, 2:3], B("OI")[:], 524288.0, 524287.0, A.mult, A.add))
        op("v", [], lambda: ts(B("C0")[:, 0:1], B("OI")[:], float(W), float(-W * rb), A.mult, A.add))
        op("v", [], lambda: ts(B("C0")[:, 2:3], B("LI")[:], float(-RR), None, A.add))
        g2 = op("v", [], lambda: ts(B("C0")[:, 4:5], B("OI")[:], float(-rb), None, A.add))
        r = op("t", [g2], lambda: mm(B("RB")[:, 0:128], T.ONES[:], B("DK")[:], True, True), bar=True)
        op("t", [], lambda: mm(B("SS")[:, 0:5], T.PM[:], B("C0")[:, 0:5], True, False), bar=True)
        op("t", [tok_g[x]], lambda: mm(B("GP")[:, 0:128], B("G")[:], T.IDN[:], True, True))
        st["R" + x] = r

    def stage2(x):
        B = lambda n: T[n + x]
        op("v", [g2c], lambda: ts(T.P16I[:], T.PI[:], 15, None, A.bitwise_and), bar=True)
        a = None
        for k, col in ((0, 2), (1, 1), (2, 0)):
            a = op("v", [st["R" + x]], lambda: ts(B("AA")[:, 128 * k:128 * k + 128], B("RB")[:, 0:128],
                                                  B("KEY")[:, col:col + 1], None, A.is_gt))
        for k in range(3):
            st["S" + x] = op("t", [a], lambda: mm(B("SS")[:, 0:5], B("AA")[:, 128 * k:128 * k + 128],
                                                  T.KC[:, 5 * k:5 * k + 5], False, k == 2))

    def stage3(x, evq):
        B = lambda n: T[n + x]
        S = B("SS")
        gt = None
        if evq == "s":
            gt = op("s", [st["S" + x]], lambda: g.scalar.activation(B("GT")[:], B("GP")[:, 0:128], cp), bar=True)
        op("v", [st["S" + x]], lambda: ts(B("SEL")[:], T.IOT[:], S[:, 0:1], None, A.is_equal), bar=True)
        if evq == "v":
            op("v", [], lambda: V.tensor_copy(B("GT")[:], B("GP")[:, 0:128]))
        g4 = op("v", [], lambda: ts(B("VV")[:], S[:, 3:4], 0.0, S[:, 2:3], A.is_equal, A.mult))
        op("t", [g4, gt], lambda: mm(B("PK")[:, 0:NS], B("GT")[:], B("SEL")[:], True, False), bar=True)
        op("v", [], lambda: ts(B("RM")[:], T.IOT[:, 0:8], S[:, 4:5], B("VV")[:, 0:1], A.is_equal, A.mult), bar=True)
        op("v", [], lambda: ts(T.P16F[:, 0:1], T.P16I[:], float(RR), None, A.add))
        op("v", [], lambda: ts(T.P16F[:, 1:2], T.P16I[:], float(RR + 16), None, A.add))
        g5 = op("v", [g3c], lambda: ts(B("LL")[:], T.PAT[:], S[:, 1:2], None, A.is_equal))
        for h in (0, 1):
            st["P" + x] = op("t", [g5], lambda: mm(B("PK")[:, 32 + h:NS:W], B("LL")[:, 128 * h:128 * h + 128],
                                                   B("RM")[:], False, h == 1))
        op("v", [], lambda: ts(T.TR[:, 32:NS:W], T.IOT[:, 0:8], 0.0, T.P16F[:, 0:1], A.mult, A.add), bar=True)
        op("v", [], lambda: ts(T.TR[:, 33:NS:W], T.IOT[:, 0:8], 0.0, T.P16F[:, 1:2], A.mult, A.add))

    def stage4(x):
        B = lambda n: T[n + x]
        st["PAY" + x] = op("v", [st["P" + x]], lambda: V.tensor_tensor(B("PAY")[:], B("PK")[:, 0:NS], T.TR[:], A.add),
                           bar=True)

    def batch(x):
        wait("g", st["PAY" + x])
        s = (0 if x == "a" else 8) + a_me
        for ks in CALLS[x]:
            trs = []
            for k in ks:
                if k == 0 and core == home:
                    continue
                b = (a_me + k) % 8
                rid, pid = topo.addr(cores[rb + b], core)
                m = part_mask(core, a_me, b)
                trs.append(RemoteDMATransfer(dst_ids=[DstId(rid=rid, pnc=pid)], dma_engine_mask=m,
                                             remote_sem=T.sem["arr%d" % s], src=T["PAY" + x][:, W * b:W * b + W],
                                             dst=T.LAND[:, W * s:W * s + W]))
                cnt["sent"] = cnt.get("sent", 0) + pop(m)
            if trs:
                g.remote_dma_fused(trs, local_sem=T.sem.sent)

    for x in sets:
        stage1(x)
        stage2(x)
        stage3(x, "v" if rank is not None else "s")
        stage4(x)
        batch(x)

    if rank is not None:
        win = T.Y[:, 0:YW]
        parts = []
        for x, base in (("a", 0), ("b", 8)):
            for ks in CALLS[x]:
                lst = []
                for k in ks:
                    a_src = (a_me - k) % 8
                    s = base + a_src
                    if k == 0 and x in sets:
                        c = W * a_me
                        lst.append((T["PAY" + x][:, c:c + 32], T["PAY" + x][:, c + 32:c + W], None))
                        continue
                    src = cores[rb + a_src] if x == "a" else worker[rb + a_src]
                    tok = expect("arr%d" % s, pop(part_mask(src, a_src, a_me)))
                    lst.append((T.LAND[:, W * s:W * s + 32], T.LAND[:, W * s + 32:W * s + W], tok))
                parts.append(lst)
        last = None
        l = 0
        for lst in parts:
            for i, (D, Fo, tok) in enumerate(lst):
                off = T.OFFU[:, 2 * (l + i):2 * (l + i) + 2]
                op("v", [tok], lambda: V.tensor_copy(off, Fo), bar=(l == 0 and i == 0))
            for D, Fo, tok in lst:
                off = T.OFFU[:, 2 * l:2 * l + 2]
                if l == 0:
                    last = op("v", [zero], lambda: V.tensor_copy(win.indirect(off), D), bar=True)
                else:
                    op("v", [], lambda: V.tensor_tensor(T.TMP[:], win.indirect(off), D, A.add), bar=True)
                    last = op("v", [], lambda: V.tensor_copy(win.indirect(off), T.TMP[:]), bar=True)
                l += 1
        wait("y", last)
        g.sync.dma_start(T.y[:], T.Y[:, 0:RR]).then_inc(T.sem.sty, 16)
        expect("sty", 16)

    for name in sorted(cnt):
        wait("g", (name, cnt[name]))
